import numpy as np
import ml_dtypes


def mxq(x, axis, fmt="e4m3"):
    dtype, down = {"e4m3": (ml_dtypes.float8_e4m3fn, 7), "e5m2": (ml_dtypes.float8_e5m2, 14)}[fmt]
    v = np.moveaxis(np.asarray(x, np.float32).astype(ml_dtypes.bfloat16).astype(np.float64), axis, -1)
    blocks = v.reshape(v.shape[:-1] + (-1, 32))
    amax = np.abs(blocks).max(-1, keepdims=True)
    byte = np.maximum(np.where(amax > 0, np.frexp(amax)[1] - 1 + 127, 0) - down, 1)
    scale = np.exp2(byte - 127.0)
    codes = (blocks / scale).astype(np.float32).astype(dtype).astype(np.float64)
    return np.moveaxis((codes * scale).reshape(v.shape), -1, axis)


WIDE = False


def mx_kscale(k):
    if not WIDE:
        return np.ones(k)
    levels = np.array([10, -10, 5, -5, 0])
    if k % 512:
        return np.exp2(np.random.permutation(np.resize(levels, k // 32))).repeat(32)
    a = np.empty((k // 512, 16))
    for p in range(k // 512):
        a[p, :8] = np.random.permutation(np.resize(levels, 8))
        for g in range(8):
            far = levels[np.abs(levels - a[p, g]) >= 10]
            a[p, g + 8] = far[np.random.randint(len(far))]
    return np.exp2(a.ravel()).repeat(32)


BF16 = ml_dtypes.bfloat16


def bf(x):
    return np.asarray(x, np.float32).astype(BF16)


def f64(x):
    return np.asarray(x).astype(np.float64)


E2M1 = np.array([0.0, 0.5, 1.0, 1.5, 2.0, 3.0, 4.0, 6.0, -0.0, -0.5, -1.0, -1.5, -2.0, -3.0, -4.0, -6.0])


def pack_weight(w, fmt):
    k, n = w.shape
    w = f64(bf(w)).reshape(k // 32, 32, n)
    amax = np.abs(w).max(1)
    if fmt == "e4m3":
        byte = np.frexp(amax)[1] - 1 + 127 - 7
    else:
        mant, ex = np.frexp(amax / 6.0)
        byte = np.where(mant > 0.5, ex, ex - 1) + 127
    byte = np.clip(np.where(amax > 0, byte, 1), 1, 254)
    scaled = (w * np.exp2(127.0 - byte)[:, None, :]).reshape(k, n).astype(np.float32)
    by_word = np.ascontiguousarray(scaled.reshape(k // 512, 128, 4, n).transpose(0, 1, 3, 2))
    if fmt == "e4m3":
        words = by_word.astype(ml_dtypes.float8_e4m3fn).view(np.uint8)
    else:
        c = by_word.astype(ml_dtypes.float4_e2m1fn).view(np.uint8) & 0xF
        words = c[..., 0::2] | (c[..., 1::2] << 4)
    return np.ascontiguousarray(words), np.ascontiguousarray(byte.astype(np.uint8).reshape(k // 512, 16, n))


def unpack_weight(words, scales, fmt):
    g, p, n, _ = words.shape
    if fmt == "e4m3":
        vals = np.ascontiguousarray(words).view(ml_dtypes.float8_e4m3fn).astype(np.float64)
    else:
        nib = np.empty((g, p, n, 4), np.uint8)
        nib[..., 0::2] = words & 0xF
        nib[..., 1::2] = words >> 4
        vals = E2M1[nib]
    vals = vals * np.repeat(np.exp2(scales.astype(np.float64) - 127.0), 8, axis=1)[..., None]
    return vals.transpose(0, 1, 3, 2).reshape(g * 512, n)
def pack4(w):
    words, scales = pack_weight(w, "e2m1")
    return words.reshape(words.shape[0], 128, -1), scales


def unpack4(words, scales):
    return unpack_weight(words.reshape(words.shape[0], 128, -1, 2), scales, "e2m1")


def planes(Y):
    n, m = Y.shape
    b = f64(bf(Y)).reshape(n // 32, 32, m)
    amax = np.abs(b).max(1)
    byte = np.clip(np.where(amax > 0, np.frexp(amax)[1] - 1 + 127 - 7, 1), 1, 254)
    codes = (b * np.exp2(127.0 - byte)[:, None, :]).reshape(n, m).astype(np.float32).astype(ml_dtypes.float8_e4m3fn).view(np.uint8)
    words = codes.reshape(n // 512, 128, 4, m).transpose(0, 1, 3, 2)
    return np.ascontiguousarray(words), np.ascontiguousarray(byte.astype(np.uint8).reshape(n // 512, 16, m))


T, KB, KO, R = 1024, 1536, 512, 2048
LOUD = 3.0
NORM = 0.8

def setup_inputs():
    s = mx_kscale(KB)
    u = mx_kscale(KO)
    radius = NORM * np.exp(0.2 * np.random.randn(T, 1)) / np.sqrt(KB + LOUD ** 2 * KO)
    q_base = radius * np.random.randn(T, KB)
    q_out = LOUD * radius * np.random.randn(T, KO)
    half_norm = 0.5 * ((q_base ** 2).sum(axis=1) + (q_out ** 2).sum(axis=1))
    w_base = np.random.randn(KB, R)
    w_out = np.random.randn(KO, R)
    w_base_words, w_base_scales = pack4(w_base / s[:, None])
    return {
        "q_base": bf(q_base * s[None, :]),
        "q_out": bf(q_out * u[None, :]),
        "w_base_words": w_base_words,
        "w_base_scales": w_base_scales,
        "w_out": bf(w_out / u[:, None]),
        "half_norm": bf(half_norm),
        "amp": bf(np.exp(0.7 * np.random.randn(R))),
    }

def reference(q_base, q_out, w_base_words, w_base_scales, w_out, half_norm, amp):
    p_base = mxq(f64(q_base), 1, "e4m3") @ unpack4(w_base_words, w_base_scales)
    p_out = mxq(f64(q_out), 1, "e4m3") @ mxq(f64(w_out), 0, "e4m3")
    y = np.exp(p_base + p_out - f64(half_norm)[:, None]) * f64(amp)[None, :]
    words, scales = planes(y.T)
    return y, words, scales

@@ -1,0 +1,302 @@
+from contextlib import ExitStack
+
+import concourse.mybir as mybir
+from concourse.masks import make_identity
+
+T, KB, KO, R = 1024, 1536, 512, 2048
+FLOPS = 2 * T * (KB + KO) * R
+
+F32 = mybir.dt.float32
+BF16 = mybir.dt.bfloat16
+I32 = mybir.dt.int32
+U32 = mybir.dt.uint32
+U8 = mybir.dt.uint8
+FP8X4 = mybir.dt.float8_e4m3fn_x4
+FP4X4 = mybir.dt.float4_e2m1fn_x4
+ACT = mybir.ActivationFunctionType
+ALU = mybir.AluOpType
+
+P = 128
+N = 512
+TILES = T // P
+GROUPS = R // N
+BASE_PASSES = KB // 512
+UNITS = TILES * GROUPS
+
+
+def tile_positive_query_features_g5_kernel(
+    tc, q_base, q_out, w_base_words, w_base_scales, w_out, half_norm, amp, out_0, out_1, out_2
+):
+    nc = tc.nc
+    with ExitStack() as ctx:
+        keep = ctx.enter_context(tc.tile_pool(name="keep", bufs=1))
+        work = ctx.enter_context(tc.tile_pool(name="work", bufs=4))
+        psum = ctx.enter_context(tc.psum_pool(name="psum", bufs=4))
+        ctx.enter_context(tc.manual_schedule())
+
+        def kept(name, count, shape, dtype):
+            return [keep.tile(shape, dtype, name=name + str(i), align_bytes=256) for i in range(count)]
+
+        ident = keep.tile([P, P], F32, align_bytes=256)
+        h_rows = keep.tile([P, P], BF16, align_bytes=256)
+        neg_h_rows = keep.tile([P, P], F32, align_bytes=256)
+        neg_h = keep.tile([P, TILES], F32, align_bytes=256)
+        table_in = keep.tile([P, 1], F32, align_bytes=256)
+        table_out = keep.tile([P, 1], F32, align_bytes=256)
+        q_raw = kept("q_raw", TILES, [P, KB + KO], BF16)
+        q_codes = kept("q_codes", TILES, [P, 4 * P], U32)
+        q_scales = kept("q_scales", TILES, [P, 4 * P], U8)
+        wb_words = kept("wb_words", GROUPS, [P, BASE_PASSES, 2 * N], U8)
+        wb_scales_first = keep.tile([P, BASE_PASSES, N], U8, align_bytes=256)
+        wb_scales_rest = keep.tile([P, BASE_PASSES, R - N], U8, align_bytes=256)
+        wo_raw = kept("wo_raw", GROUPS, [P, 4, N], BF16)
+        wo_grouped = kept("wo_grouped", GROUPS, [P, N, 4], BF16)
+        wo_codes = kept("wo_codes", GROUPS, [P, N], U32)
+        wo_scales = kept("wo_scales", GROUPS, [P, N], U8)
+        amp_all = kept("amp_all", GROUPS, [P, N], BF16)
+        y_codes = kept("y_codes", GROUPS, [P, T], U32)
+        y_scales = kept("y_scales", GROUPS, [P, T], U8)
+
+        acc, exps, ys, y_halves, grouped = {}, {}, {}, {}, {}
+
+        def cols(g):
+            return slice(N * g, N * (g + 1))
+
+        def load_q(t):
+            rows = slice(P * t, P * (t + 1))
+            nc.sync.dma_start(out=q_raw[t][:, :KB], in_=q_base[rows, :])
+            nc.sync.dma_start(out=q_raw[t][:, KB:], in_=q_out[rows, :])
+
+        def load_wb_scales(plane, columns):
+            for quad in range(4):
+                nc.sync.dma_start(
+                    out=plane[32 * quad : 32 * quad + 4, :, :].bitcast(I32),
+                    in_=w_base_scales[:, 4 * quad : 4 * quad + 4, columns].rearrange("c r n -> r c n").bitcast(I32),
+                )
+
+        def load_wb_words(g):
+            nc.sync.dma_start(
+                out=wb_words[g][:].bitcast(I32),
+                in_=w_base_words[:, :, 2 * N * g : 2 * N * (g + 1)].rearrange("c p n -> p c n").bitcast(I32),
+            )
+
+        def load_wo(g):
+            nc.sync.dma_start(out=wo_raw[g][:], in_=w_out[:, cols(g)].rearrange("(p j) n -> p j n", j=4))
+
+        def load_amp(g):
+            nc.sync.dma_start(out=amp_all[g][:], in_=amp[cols(g)].partition_broadcast(P))
+
+        def interleave_wo(g, part, parts, on_scalar):
+            width = N // parts
+            c = slice(width * part, width * (part + 1))
+            dst = wo_grouped[g][:, c, :].rearrange("p (c i) t -> p c t i", i=4)
+            src = wo_raw[g][:, :, c].rearrange("p t (c i) -> p c t i", i=4)
+            if on_scalar:
+                nc.scalar.copy(out=dst, in_=src)
+            else:
+                nc.vector.tensor_copy(out=dst, in_=src)
+
+        def quantize_wo(g):
+            nc.vector.quantize_mx(
+                out=wo_codes[g][:].bitcast(FP8X4),
+                scales=wo_scales[g][:],
+                in_=wo_grouped[g][:].rearrange("p n t -> p (n t)"),
+            )
+
+        def turn(key, blocks):
+            count = len(blocks) // 2
+            bank = psum.tile([P, 2, 2, P], F32, name="turn_bank")
+            for i, block in enumerate(blocks):
+                nc.tensor.transpose(bank[:, i // 2, i % 2, :], block, ident[:])
+            tile = work.tile([P, 2, P, 4], BF16, name="turned", align_bytes=256)
+            nc.scalar.copy(
+                out=tile[:, :count].bitcast(F32),
+                in_=bank[:, :count].rearrange("p c u r -> p c r u"),
+            )
+            grouped[key] = tile[:, :count].rearrange("p c r t -> p (c r t)")
+
+        def turn_q(t, half):
+            words = q_raw[t][:].bitcast(F32)
+            turn(("q", t, half), [words[:, 256 * c + u : 256 * (c + 1) : 2] for c in (2 * half, 2 * half + 1) for u in (0, 1)])
+
+        def quantize_q(t, half):
+            c = slice(2 * P * half, 2 * P * (half + 1))
+            nc.vector.quantize_mx(out=q_codes[t][:, c].bitcast(FP8X4), scales=q_scales[t][:, c], in_=grouped["q", t, half])
+
+        def multiply(n, passes):
+            g, t = divmod(n, TILES)
+            if n not in acc:
+                acc[n] = psum.tile([P, N], F32, name="acc")
+            for c in passes:
+                q_cols = slice(P * c, P * (c + 1))
+                if c < BASE_PASSES:
+                    rhs = wb_words[g][:, c, :].bitcast(FP4X4)
+                    rhs_scale = wb_scales_first[:, c, :] if g == 0 else wb_scales_rest[:, c, cols(g - 1)]
+                else:
+                    rhs = wo_codes[g][:].bitcast(FP8X4)
+                    rhs_scale = wo_scales[g][:]
+                nc.tensor.matmul_mx(
+                    out=acc[n][:],
+                    lhsT=q_codes[t][:, q_cols].bitcast(FP8X4),
+                    lhsT_scale=q_scales[t][:, q_cols],
+                    rhs=rhs,
+                    rhs_scale=rhs_scale,
+                    start=(c == 0),
+                    stop=(c == BASE_PASSES),
+                )
+
+        def exponential(n):
+            t = n % TILES
+            exps[n] = work.tile([P, N], F32, name="exp")
+            nc.scalar.activation(out=exps[n][:], in_=acc[n][:], func=ACT.Exp, bias=neg_h[:, t : t + 1])
+
+        def amplify(n):
+            g, t = divmod(n, TILES)
+            ys[n] = work.tile([P, N], F32, name="y", bufs=14)
+            nc.vector.tensor_tensor(out=ys[n][:], in0=exps[n][:], in1=amp_all[g][:], op=ALU.mult)
+
+        def store_y(n):
+            g, t = divmod(n, TILES)
+            nc.sync.dma_start(out=out_0[P * t : P * (t + 1), cols(g)], in_=ys[n][:])
+
+        def round_y(n):
+            y_halves[n] = work.tile([P, 2, P, 2], BF16, name="y_halves", bufs=10, align_bytes=256)
+            nc.vector.tensor_copy(out=y_halves[n][:], in_=ys[n][:].rearrange("p (m u e) -> p u m e", u=2, e=2))
+
+        def turn_y(units):
+            blocks = [y_halves[n][:, u].rearrange("p m e -> p (m e)").bitcast(F32) for n in units for u in (0, 1)]
+            turn(("y", units), blocks)
+
+        def quantize_y(units):
+            g, t = divmod(units[0], TILES)
+            c = slice(P * t, P * (t + len(units)))
+            nc.vector.quantize_mx(out=y_codes[g][:, c].bitcast(FP8X4), scales=y_scales[g][:, c], in_=grouped["y", units])
+
+        def store_words(g, t0, t1):
+            nc.sync.dma_start(
+                out=out_1[g].rearrange("p m t -> p (m t)")[:, 4 * P * t0 : 4 * P * t1].bitcast(I32),
+                in_=y_codes[g][:, P * t0 : P * t1].bitcast(I32),
+            )
+
+        def store_scales(g, queues):
+            for quad, queue in enumerate(queues):
+                queue.dma_start(
+                    out=out_2[g, 4 * quad : 4 * quad + 4, :].bitcast(I32),
+                    in_=y_scales[g][32 * quad : 32 * quad + 4, :].bitcast(I32),
+                )
+
+        nc.vector.memset(h_rows[:], 0.0)
+        nc.vector.memset(wb_scales_first[:].bitcast(I32), 0)
+        nc.vector.memset(table_in[:], 0.0)
+        nc.vector.memset(wb_scales_rest[:].bitcast(I32), 0)
+        make_identity(nc, ident[:])
+        nc.scalar.activation(out=table_out[:], in_=table_in[:], func=ACT.Exp)
+
+        load_q(0)
+        load_q(1)
+        load_wb_words(0)
+        load_wb_scales(wb_scales_first, cols(0))
+        load_wo(0)
+        nc.sync.dma_start(out=h_rows[:TILES, :], in_=half_norm.rearrange("(a n) -> a n", n=P))
+        load_q(2)
+        load_amp(0)
+        for t in range(3, TILES):
+            load_q(t)
+        load_wo(1)
+        load_wb_scales(wb_scales_rest, slice(N, R))
+        load_wb_words(1)
+        load_amp(1)
+        for g in range(2, GROUPS):
+            load_wo(g)
+            load_wb_words(g)
+            load_amp(g)
+
+        for t in (0, 1):
+            for half in (0, 1):
+                turn_q(t, half)
+                quantize_q(t, half)
+        multiply(0, range(BASE_PASSES))
+        multiply(1, range(BASE_PASSES))
+        interleave_wo(0, 3, 4, True)
+        nc.vector.tensor_scalar(out=neg_h_rows[:], in0=h_rows[:], scalar1=-1.0, scalar2=None, op0=ALU.mult)
+        for part in range(3):
+            interleave_wo(0, part, 4, False)
+        h_bank = psum.tile([P, 2, 2, P], F32, name="turn_bank")
+        nc.tensor.transpose(h_bank[:, 0, 0, :], neg_h_rows[:], ident[:])
+        nc.scalar.copy(out=neg_h[:], in_=h_bank[:, 0, 0, :TILES])
+        turn_q(2, 0)
+        turn_q(2, 1)
+        quantize_wo(0)
+        quantize_q(2, 0)
+        quantize_q(2, 1)
+        multiply(0, [BASE_PASSES])
+        exponential(0)
+        multiply(1, [BASE_PASSES])
+        exponential(1)
+        amplify(0)
+        store_y(0)
+
+        next_pair = 0
+        for n in range(2, UNITS):
+            g, t = divmod(n, TILES)
+            q_next = n + 1 if n + 1 < TILES else None
+            pairs = []
+            if (n % 2 == 1 if n < TILES else n % 4 == 3):
+                while next_pair + 1 <= n - 4:
+                    pairs.append((next_pair, next_pair + 1))
+                    next_pair += 2
+            if q_next is not None:
+                turn_q(q_next, 0)
+                turn_q(q_next, 1)
+            for pair in pairs:
+                turn_y(pair)
+            multiply(n, range(BASE_PASSES + 1))
+            amplify(n - 1)
+            round_y(n - 2)
+            if q_next is not None:
+                quantize_q(q_next, 0)
+                quantize_q(q_next, 1)
+            for pair in pairs:
+                quantize_y(pair)
+            if g == 0 and t in (5, 6):
+                interleave_wo(1, 2 * (t - 5), 4, False)
+                interleave_wo(1, 2 * (t - 5) + 1, 4, t == 6)
+            if g == 0 and t == 7:
+                quantize_wo(1)
+            if 0 < g < GROUPS - 1:
+                if t in (0, 1, 4, 5):
+                    interleave_wo(g + 1, (0, 1, 4, 5).index(t), 4, True)
+                if t == 6:
+                    quantize_wo(g + 1)
+            if n < UNITS - 1:
+                exponential(n)
+            store_y(n - 1)
+            for pair in pairs:
+                if pair[1] % TILES == TILES - 1:
+                    store_words(pair[1] // TILES, 0, TILES)
+                    store_scales(pair[1] // TILES, (nc.sync,) * 4)
+
+        last = UNITS - 1
+        g, t = divmod(last, TILES)
+        store_words(g, 0, TILES - 4)
+        round_y(last - 1)
+        exps[last] = work.tile([P, N], F32, name="exp")
+        y_halves[last] = work.tile([P, 2, P, 2], BF16, name="y_halves", bufs=10, align_bytes=256)
+        for half in (0, 1):
+            c = slice(N // 2 * half, N // 2 * (half + 1))
+            nc.scalar.activation(out=exps[last][:, c], in_=acc[last][:, c], func=ACT.Exp, bias=neg_h[:, t : t + 1])
+            nc.vector.tensor_tensor(
+                out=y_halves[last][:, :, P // 2 * half : P // 2 * (half + 1), :],
+                in0=exps[last][:, c].rearrange("p (m u e) -> p u m e", u=2, e=2),
+                in1=amp_all[g][:, c].rearrange("p (m u e) -> p u m e", u=2, e=2),
+                op=ALU.mult,
+            )
+        turn_y((last - 3, last - 2))
+        turn_y((last - 1, last))
+        amplify(last)
+        store_y(last)
+        quantize_y((last - 3, last - 2))
+        store_words(g, TILES - 4, TILES - 2)
+        quantize_y((last - 1, last))
+        store_words(g, TILES - 2, TILES)
+        store_scales(g, (nc.sync, nc.sync, nc.scalar, nc.scalar))

@@ -22,6 +22,9 @@ TILES = T // P
 GROUPS = R // N
 BASE_PASSES = KB // 512
 UNITS = TILES * GROUPS
+PHASES = GROUPS // 2
+WO_ON_SCALAR = {7: 0, 9: 1, 11: 4, 13: 5}
+WO_ON_VECTOR = {7: 2, 9: 3, 11: 6, 13: 7}
 
 
 def tile_positive_query_features_g5_kernel(
@@ -38,8 +41,9 @@ def tile_positive_query_features_g5_kernel(
             return [keep.tile(shape, dtype, name=name + str(i), align_bytes=256) for i in range(count)]
 
         ident = keep.tile([P, P], F32, align_bytes=256)
-        h_rows = keep.tile([P, P], BF16, align_bytes=256)
-        neg_h_rows = keep.tile([P, P], F32, align_bytes=256)
+        ident_bf16 = keep.tile([P, P], BF16, align_bytes=256)
+        vector_rows = keep.tile([P, P], BF16, align_bytes=256)
+        amp_cols = keep.tile([P, R // P], BF16, align_bytes=256)
         neg_h = keep.tile([P, TILES], F32, align_bytes=256)
         table_in = keep.tile([P, 1], F32, align_bytes=256)
         table_out = keep.tile([P, 1], F32, align_bytes=256)
@@ -47,20 +51,24 @@ def tile_positive_query_features_g5_kernel(
         q_codes = kept("q_codes", TILES, [P, 4 * P], U32)
         q_scales = kept("q_scales", TILES, [P, 4 * P], U8)
         wb_words = kept("wb_words", GROUPS, [P, BASE_PASSES, 2 * N], U8)
-        wb_scales_first = keep.tile([P, BASE_PASSES, N], U8, align_bytes=256)
-        wb_scales_rest = keep.tile([P, BASE_PASSES, R - N], U8, align_bytes=256)
+        wb_scales = kept("wb_scales", 2, [P, BASE_PASSES, N], U8)
+        wb_scales_late = keep.tile([P, BASE_PASSES, 2 * N], U8, align_bytes=256)
         wo_raw = kept("wo_raw", GROUPS, [P, 4, N], BF16)
         wo_grouped = kept("wo_grouped", GROUPS, [P, N, 4], BF16)
         wo_codes = kept("wo_codes", GROUPS, [P, N], U32)
         wo_scales = kept("wo_scales", GROUPS, [P, N], U8)
         amp_all = kept("amp_all", GROUPS, [P, N], BF16)
-        y_codes = kept("y_codes", GROUPS, [P, T], U32)
-        y_scales = kept("y_scales", GROUPS, [P, T], U8)
+        y_codes = kept("y_codes", PHASES, [P, 2, T], U32)
+        y_scales = kept("y_scales", PHASES, [P, T], U8)
 
         acc, exps, ys, y_halves, grouped = {}, {}, {}, {}, {}
 
         def cols(g):
             return slice(N * g, N * (g + 1))
+
+        def place(n):
+            phase, rest = divmod(n, 2 * TILES)
+            return 2 * phase + rest % 2, rest // 2
 
         def load_q(t):
             rows = slice(P * t, P * (t + 1))
@@ -83,8 +91,12 @@ def tile_positive_query_features_g5_kernel(
         def load_wo(g):
             nc.sync.dma_start(out=wo_raw[g][:], in_=w_out[:, cols(g)].rearrange("(p j) n -> p j n", j=4))
 
-        def load_amp(g):
-            nc.sync.dma_start(out=amp_all[g][:], in_=amp[cols(g)].partition_broadcast(P))
+        def spread_amp(g):
+            bank = psum.tile([P, 4, P], BF16, name="turn_bank")
+            for i in range(4):
+                column = amp_cols[:, 4 * g + i : 4 * g + i + 1]
+                nc.tensor.transpose(bank[:, i, :], column.to_broadcast([P, P]), ident_bf16[:])
+            nc.scalar.copy(out=amp_all[g][:], in_=bank[:].rearrange("p i n -> p (i n)"))
 
         def interleave_wo(g, part, parts, on_scalar):
             width = N // parts
@@ -113,7 +125,7 @@ def tile_positive_query_features_g5_kernel(
                 out=tile[:, :count].bitcast(F32),
                 in_=bank[:, :count].rearrange("p c u r -> p c r u"),
             )
-            grouped[key] = tile[:, :count].rearrange("p c r t -> p (c r t)")
+            grouped[key] = tile
 
         def turn_q(t, half):
             words = q_raw[t][:].bitcast(F32)
@@ -121,17 +133,17 @@ def tile_positive_query_features_g5_kernel(
 
         def quantize_q(t, half):
             c = slice(2 * P * half, 2 * P * (half + 1))
-            nc.vector.quantize_mx(out=q_codes[t][:, c].bitcast(FP8X4), scales=q_scales[t][:, c], in_=grouped["q", t, half])
+            nc.vector.quantize_mx(out=q_codes[t][:, c].bitcast(FP8X4), scales=q_scales[t][:, c], in_=grouped["q", t, half][:].rearrange("p c r t -> p (c r t)"))
 
         def multiply(n, passes):
-            g, t = divmod(n, TILES)
+            g, t = place(n)
             if n not in acc:
                 acc[n] = psum.tile([P, N], F32, name="acc")
             for c in passes:
                 q_cols = slice(P * c, P * (c + 1))
                 if c < BASE_PASSES:
                     rhs = wb_words[g][:, c, :].bitcast(FP4X4)
-                    rhs_scale = wb_scales_first[:, c, :] if g == 0 else wb_scales_rest[:, c, cols(g - 1)]
+                    rhs_scale = wb_scales[g][:, c, :] if g < 2 else wb_scales_late[:, c, cols(g - 2)]
                 else:
                     rhs = wo_codes[g][:].bitcast(FP8X4)
                     rhs_scale = wo_scales[g][:]
@@ -146,140 +158,189 @@ def tile_positive_query_features_g5_kernel(
                 )
 
         def exponential(n):
-            t = n % TILES
+            g, t = place(n)
             exps[n] = work.tile([P, N], F32, name="exp")
             nc.scalar.activation(out=exps[n][:], in_=acc[n][:], func=ACT.Exp, bias=neg_h[:, t : t + 1])
 
         def amplify(n):
-            g, t = divmod(n, TILES)
-            ys[n] = work.tile([P, N], F32, name="y", bufs=14)
-            nc.vector.tensor_tensor(out=ys[n][:], in0=exps[n][:], in1=amp_all[g][:], op=ALU.mult)
+            g, t = place(n)
+            if n % 2 == 0:
+                ys[n // 2] = work.tile([P, 2, N], F32, name="y", bufs=7)
+            nc.vector.tensor_tensor(out=ys[n // 2][:, n % 2, :], in0=exps[n][:], in1=amp_all[g][:], op=ALU.mult)
 
-        def store_y(n):
-            g, t = divmod(n, TILES)
-            nc.sync.dma_start(out=out_0[P * t : P * (t + 1), cols(g)], in_=ys[n][:])
+        def store_y(n, count):
+            g, t = place(n)
+            nc.sync.dma_start(
+                out=out_0[P * t : P * (t + 1), N * g : N * (g + count)],
+                in_=ys[n // 2][:, n % 2 : n % 2 + count, :].rearrange("p a n -> p (a n)"),
+            )
 
         def round_y(n):
             y_halves[n] = work.tile([P, 2, P, 2], BF16, name="y_halves", bufs=10, align_bytes=256)
-            nc.vector.tensor_copy(out=y_halves[n][:], in_=ys[n][:].rearrange("p (m u e) -> p u m e", u=2, e=2))
-
-        def turn_y(units):
-            blocks = [y_halves[n][:, u].rearrange("p m e -> p (m e)").bitcast(F32) for n in units for u in (0, 1)]
-            turn(("y", units), blocks)
-
-        def quantize_y(units):
-            g, t = divmod(units[0], TILES)
-            c = slice(P * t, P * (t + len(units)))
-            nc.vector.quantize_mx(out=y_codes[g][:, c].bitcast(FP8X4), scales=y_scales[g][:, c], in_=grouped["y", units])
-
-        def store_words(g, t0, t1):
-            nc.sync.dma_start(
-                out=out_1[g].rearrange("p m t -> p (m t)")[:, 4 * P * t0 : 4 * P * t1].bitcast(I32),
-                in_=y_codes[g][:, P * t0 : P * t1].bitcast(I32),
+            nc.vector.tensor_copy(
+                out=y_halves[n][:], in_=ys[n // 2][:, n % 2, :].rearrange("p (m u e) -> p u m e", u=2, e=2)
             )
 
-        def store_scales(g, queues):
+        def turn_y(units):
+            blocks = [y_halves[m][:, u].rearrange("p m e -> p (m e)").bitcast(F32) for m in units for u in (0, 1)]
+            turn("y", blocks)
+            for i, m in enumerate(units):
+                grouped["y", m] = grouped["y"][:, i]
+
+        def quantize_y(n):
+            g, t = place(n)
+            c = slice(P * t, P * (t + 1))
+            nc.vector.quantize_mx(
+                out=y_codes[g // 2][:, g % 2, c].bitcast(FP8X4),
+                scales=y_scales[g // 2][4 * (g % 2) :, c],
+                in_=grouped["y", n].rearrange("p r t -> p (r t)"),
+            )
+
+        def store_words(phase, t0, t1):
+            words = out_1[2 * phase : 2 * phase + 2].rearrange("g p m t -> p g (m t)")
+            nc.sync.dma_start(
+                out=words[:, :, 4 * P * t0 : 4 * P * t1].bitcast(I32),
+                in_=y_codes[phase][:, :, P * t0 : P * t1].bitcast(I32),
+            )
+
+        def store_scales(phase, t0, t1, queues):
             for quad, queue in enumerate(queues):
                 queue.dma_start(
-                    out=out_2[g, 4 * quad : 4 * quad + 4, :].bitcast(I32),
-                    in_=y_scales[g][32 * quad : 32 * quad + 4, :].bitcast(I32),
+                    out=out_2[2 * phase : 2 * phase + 2, 4 * quad : 4 * quad + 4, P * t0 : P * t1].bitcast(I32),
+                    in_=y_scales[phase][32 * quad : 32 * quad + 8, P * t0 : P * t1].bitcast(I32),
                 )
 
-        nc.vector.memset(h_rows[:], 0.0)
-        nc.vector.memset(wb_scales_first[:].bitcast(I32), 0)
+        nc.vector.memset(vector_rows[:], 0.0)
+        nc.vector.memset(wb_scales[0][:].bitcast(I32), 0)
         nc.vector.memset(table_in[:], 0.0)
-        nc.vector.memset(wb_scales_rest[:].bitcast(I32), 0)
+        nc.vector.memset(wb_scales[1][:].bitcast(I32), 0)
+        nc.vector.memset(wb_scales_late[:].bitcast(I32), 0)
         make_identity(nc, ident[:])
+        make_identity(nc, ident_bf16[:])
         nc.scalar.activation(out=table_out[:], in_=table_in[:], func=ACT.Exp)
 
         load_q(0)
+        nc.sync.dma_start(out=vector_rows[:TILES, :], in_=half_norm.rearrange("(a n) -> a n", n=P))
+        nc.sync.dma_start(out=vector_rows[32 : 32 + R // P, :], in_=amp.rearrange("(a n) -> a n", n=P))
         load_q(1)
         load_wb_words(0)
-        load_wb_scales(wb_scales_first, cols(0))
+        load_wb_scales(wb_scales[0], cols(0))
         load_wo(0)
-        nc.sync.dma_start(out=h_rows[:TILES, :], in_=half_norm.rearrange("(a n) -> a n", n=P))
-        load_q(2)
-        load_amp(0)
-        for t in range(3, TILES):
-            load_q(t)
-        load_wo(1)
-        load_wb_scales(wb_scales_rest, slice(N, R))
         load_wb_words(1)
-        load_amp(1)
-        for g in range(2, GROUPS):
-            load_wo(g)
-            load_wb_words(g)
-            load_amp(g)
+        load_wb_scales(wb_scales[1], cols(1))
+        load_wo(1)
+        for t in range(2, TILES):
+            load_q(t)
+        load_wo(2)
+        load_wo(3)
+        load_wb_scales(wb_scales_late, slice(2 * N, R))
+        load_wb_words(2)
+        load_wb_words(3)
 
-        for t in (0, 1):
-            for half in (0, 1):
-                turn_q(t, half)
-                quantize_q(t, half)
+        turn_q(0, 0)
+        turn_q(0, 1)
+        vector_bank = psum.tile([P, P], BF16, name="turn_bank")
+        nc.tensor.transpose(vector_bank[:], vector_rows[:], ident_bf16[:])
+        nc.vector.tensor_copy(out=amp_cols[:], in_=vector_bank[:, 32 : 32 + R // P])
+        nc.vector.tensor_scalar(out=neg_h[:], in0=vector_bank[:, :TILES], scalar1=-1.0, scalar2=None, op0=ALU.mult)
+        quantize_q(0, 0)
+        quantize_q(0, 1)
+        for half in (0, 1):
+            turn_q(1, half)
+            quantize_q(1, half)
+        for g in range(GROUPS):
+            spread_amp(g)
         multiply(0, range(BASE_PASSES))
-        multiply(1, range(BASE_PASSES))
+        multiply(2, range(BASE_PASSES))
         interleave_wo(0, 3, 4, True)
-        nc.vector.tensor_scalar(out=neg_h_rows[:], in0=h_rows[:], scalar1=-1.0, scalar2=None, op0=ALU.mult)
         for part in range(3):
             interleave_wo(0, part, 4, False)
-        h_bank = psum.tile([P, 2, 2, P], F32, name="turn_bank")
-        nc.tensor.transpose(h_bank[:, 0, 0, :], neg_h_rows[:], ident[:])
-        nc.scalar.copy(out=neg_h[:], in_=h_bank[:, 0, 0, :TILES])
+        quantize_wo(0)
+        multiply(1, range(BASE_PASSES))
+        multiply(0, [BASE_PASSES])
+        multiply(2, [BASE_PASSES])
+        multiply(3, range(BASE_PASSES))
+        interleave_wo(1, 3, 4, True)
+        for part in range(3):
+            interleave_wo(1, part, 4, False)
+        exponential(0)
+        exponential(2)
+        amplify(0)
+        quantize_wo(1)
         turn_q(2, 0)
         turn_q(2, 1)
-        quantize_wo(0)
+        multiply(1, [BASE_PASSES])
+        multiply(3, [BASE_PASSES])
+        amplify(2)
+        round_y(0)
         quantize_q(2, 0)
         quantize_q(2, 1)
-        multiply(0, [BASE_PASSES])
-        exponential(0)
-        multiply(1, [BASE_PASSES])
         exponential(1)
-        amplify(0)
-        store_y(0)
+        exponential(3)
+        amplify(1)
+        round_y(2)
+        store_y(0, 2)
 
         next_pair = 0
-        for n in range(2, UNITS):
-            g, t = divmod(n, TILES)
-            q_next = n + 1 if n + 1 < TILES else None
+        waiting = []
+        for n in range(4, UNITS):
+            g, t = place(n)
+            first_phase = n < 2 * TILES
+            q_next = t + 1 if first_phase and n % 2 == 0 and t + 1 < TILES else None
             pairs = []
-            if (n % 2 == 1 if n < TILES else n % 4 == 3):
-                while next_pair + 1 <= n - 4:
-                    pairs.append((next_pair, next_pair + 1))
+            if (n % 2 == 0 if first_phase else n % 4 == 1 or n == UNITS - 1):
+                while next_pair + 1 <= (n - 3 if q_next is not None and n > 4 else n - 4):
+                    pairs.append(next_pair)
                     next_pair += 2
             if q_next is not None:
                 turn_q(q_next, 0)
                 turn_q(q_next, 1)
             for pair in pairs:
-                turn_y(pair)
+                turn_y((pair, pair + 1))
             multiply(n, range(BASE_PASSES + 1))
             amplify(n - 1)
-            round_y(n - 2)
+            if waiting:
+                quantize_y(waiting.pop(0))
+            round_y(1 if n == 4 else n - 2)
             if q_next is not None:
                 quantize_q(q_next, 0)
                 quantize_q(q_next, 1)
             for pair in pairs:
                 quantize_y(pair)
-            if g == 0 and t in (5, 6):
-                interleave_wo(1, 2 * (t - 5), 4, False)
-                interleave_wo(1, 2 * (t - 5) + 1, 4, t == 6)
-            if g == 0 and t == 7:
-                quantize_wo(1)
-            if 0 < g < GROUPS - 1:
-                if t in (0, 1, 4, 5):
-                    interleave_wo(g + 1, (0, 1, 4, 5).index(t), 4, True)
-                if t == 6:
-                    quantize_wo(g + 1)
+            for pair in pairs:
+                if len(pairs) > 1:
+                    quantize_y(pair + 1)
+                else:
+                    waiting.append(pair + 1)
+            if n in WO_ON_SCALAR:
+                part = WO_ON_SCALAR[n]
+                interleave_wo(2 + part // 4, part % 4, 4, True)
+            if n in WO_ON_VECTOR:
+                part = WO_ON_VECTOR[n]
+                interleave_wo(2 + part // 4, part % 4, 4, False)
+            if n in (12, 14):
+                quantize_wo(2 + (n - 12) // 2)
             if n < UNITS - 1:
                 exponential(n)
-            store_y(n - 1)
-            for pair in pairs:
-                if pair[1] % TILES == TILES - 1:
-                    store_words(pair[1] // TILES, 0, TILES)
-                    store_scales(pair[1] // TILES, (nc.sync,) * 4)
+            if n % 2 == 0:
+                store_y(n - 2, 2)
+            if n == 22:
+                store_words(0, 4, TILES)
+                store_scales(0, 0, TILES, (nc.sync,) * 4)
+            if n == 14:
+                store_words(0, 0, 4)
+            if n == 26:
+                store_words(1, 0, 3)
+            if n == 29:
+                store_words(1, 3, 5)
+                store_scales(1, 0, 5, (nc.sync,) * 4)
 
         last = UNITS - 1
-        g, t = divmod(last, TILES)
-        store_words(g, 0, TILES - 4)
+        g, t = place(last)
+        store_y(last - 1, 1)
         round_y(last - 1)
+        quantize_y(waiting.pop(0))
+        store_words(1, 5, 6)
         exps[last] = work.tile([P, N], F32, name="exp")
         y_halves[last] = work.tile([P, 2, P, 2], BF16, name="y_halves", bufs=10, align_bytes=256)
         for half in (0, 1):
@@ -292,11 +353,14 @@ def tile_positive_query_features_g5_kernel(
                 op=ALU.mult,
             )
         turn_y((last - 3, last - 2))
-        turn_y((last - 1, last))
+        turn_y((last - 1,))
+        turn_y((last,))
         amplify(last)
-        store_y(last)
-        quantize_y((last - 3, last - 2))
-        store_words(g, TILES - 4, TILES - 2)
-        quantize_y((last - 1, last))
-        store_words(g, TILES - 2, TILES)
-        store_scales(g, (nc.sync, nc.sync, nc.scalar, nc.scalar))
+        store_y(last, 1)
+        quantize_y(last - 3)
+        quantize_y(last - 1)
+        quantize_y(last - 2)
+        store_words(1, 6, 7)
+        quantize_y(last)
+        store_words(1, 7, TILES)
+        store_scales(1, 5, TILES, (nc.scalar, nc.sync, nc.scalar, nc.sync))

@@ -23,8 +23,18 @@ GROUPS = R // N
 BASE_PASSES = KB // 512
 UNITS = TILES * GROUPS
 PHASES = GROUPS // 2
-WO_ON_SCALAR = {7: 0, 9: 1, 11: 4, 13: 5}
-WO_ON_VECTOR = {7: 2, 9: 3, 11: 6, 13: 7}
+WARM_PASSES = 16
+Q_TURN = {6: 4, 8: 5, 10: 6, 12: 7}
+Q_SPLIT = {6: 5, 7: 6, 9: 7}
+HEAD_EPILOGUES = 1
+CATCH_UP = (16, 18, 19, 20)
+Y_LAG = 2
+ROUND_ON_SCALAR = (13, 15, 17, 19, 21)
+Y_TURN = {10: 1, 12: 1, 17: 4, 22: 4, 26: 4, 29: 2, 31: 1}
+PLANE_STORES = ((0, 0, 2, False), (0, 2, 4, False), (0, 4, 6, False), (0, 6, 8, True), (1, 0, 2, False), (1, 2, 4, True), (1, 4, 6, False))
+WO_ON_SCALAR = {7: 0, 9: 1, 11: 2, 13: 4, 14: 5, 15: 6}
+WO_ON_VECTOR = {11: 3, 13: 7}
+WO_QUANTIZE = {14: 2, 15: 3}
 
 
 def tile_positive_query_features_g5_kernel(
@@ -61,7 +71,11 @@ def tile_positive_query_features_g5_kernel(
         y_codes = kept("y_codes", PHASES, [P, 2, T], U32)
         y_scales = kept("y_scales", PHASES, [P, T], U8)
 
-        acc, exps, ys, y_halves, grouped = {}, {}, {}, {}, {}
+        warm_in = keep.tile([P, 4 * P], BF16, align_bytes=256)
+        warm_codes = keep.tile([P, P], U32, align_bytes=256)
+        warm_scales = keep.tile([P, P], U8, align_bytes=256)
+
+        acc, exps, ys, y_halves, q_halves, grouped = {}, {}, {}, {}, {}, {}
 
         def cols(g):
             return slice(N * g, N * (g + 1))
@@ -127,9 +141,13 @@ def tile_positive_query_features_g5_kernel(
             )
             grouped[key] = tile
 
+        def split_q(t, half):
+            words = q_raw[t][:].bitcast(F32)[:, 4 * P * half : 4 * P * (half + 1)]
+            q_halves[t, half] = work.tile([P, 2, 2, P], F32, name="q_halves", bufs=6, align_bytes=256)
+            nc.vector.tensor_copy(out=q_halves[t, half][:], in_=words.rearrange("p (c m u) -> p c u m", c=2, u=2))
+
         def turn_q(t, half):
-            words = q_raw[t][:].bitcast(F32)
-            turn(("q", t, half), [words[:, 256 * c + u : 256 * (c + 1) : 2] for c in (2 * half, 2 * half + 1) for u in (0, 1)])
+            turn(("q", t, half), [q_halves[t, half][:, c, u, :] for c in (0, 1) for u in (0, 1)])
 
         def quantize_q(t, half):
             c = slice(2 * P * half, 2 * P * (half + 1))
@@ -159,12 +177,12 @@ def tile_positive_query_features_g5_kernel(
 
         def exponential(n):
             g, t = place(n)
-            exps[n] = work.tile([P, N], F32, name="exp")
+            exps[n] = work.tile([P, N], F32, name="exp", bufs=9)
             nc.scalar.activation(out=exps[n][:], in_=acc[n][:], func=ACT.Exp, bias=neg_h[:, t : t + 1])
 
         def amplify(n):
             g, t = place(n)
-            if n % 2 == 0:
+            if n // 2 not in ys:
                 ys[n // 2] = work.tile([P, 2, N], F32, name="y", bufs=7)
             nc.vector.tensor_tensor(out=ys[n // 2][:, n % 2, :], in0=exps[n][:], in1=amp_all[g][:], op=ALU.mult)
 
@@ -177,9 +195,8 @@ def tile_positive_query_features_g5_kernel(
 
         def round_y(n):
             y_halves[n] = work.tile([P, 2, P, 2], BF16, name="y_halves", bufs=10, align_bytes=256)
-            nc.vector.tensor_copy(
-                out=y_halves[n][:], in_=ys[n // 2][:, n % 2, :].rearrange("p (m u e) -> p u m e", u=2, e=2)
-            )
+            copy = nc.scalar.copy if n in ROUND_ON_SCALAR else nc.vector.tensor_copy
+            copy(out=y_halves[n][:], in_=ys[n // 2][:, n % 2, :].rearrange("p (m u e) -> p u m e", u=2, e=2))
 
         def turn_y(units):
             blocks = [y_halves[m][:, u].rearrange("p m e -> p (m e)").bitcast(F32) for m in units for u in (0, 1)]
@@ -210,7 +227,9 @@ def tile_positive_query_features_g5_kernel(
                     in_=y_scales[phase][32 * quad : 32 * quad + 8, P * t0 : P * t1].bitcast(I32),
                 )
 
+        nc.vector.memset(warm_in[:].bitcast(I32), 0)
         nc.vector.memset(vector_rows[:], 0.0)
+        nc.vector.quantize_mx(out=warm_codes[:].bitcast(FP8X4), scales=warm_scales[:], in_=warm_in[:])
         nc.vector.memset(wb_scales[0][:].bitcast(I32), 0)
         nc.vector.memset(table_in[:], 0.0)
         nc.vector.memset(wb_scales[1][:].bitcast(I32), 0)
@@ -226,10 +245,11 @@ def tile_positive_query_features_g5_kernel(
         load_wb_words(0)
         load_wb_scales(wb_scales[0], cols(0))
         load_wo(0)
+        load_q(2)
         load_wb_words(1)
         load_wb_scales(wb_scales[1], cols(1))
         load_wo(1)
-        for t in range(2, TILES):
+        for t in range(3, TILES):
             load_q(t)
         load_wo(2)
         load_wo(3)
@@ -237,79 +257,133 @@ def tile_positive_query_features_g5_kernel(
         load_wb_words(2)
         load_wb_words(3)
 
-        turn_q(0, 0)
-        turn_q(0, 1)
+        warm_bank = psum.tile([P, N], F32, name="acc")
+        for i in range(WARM_PASSES):
+            nc.tensor.matmul_mx(
+                out=warm_bank[:, P * (i % 4) : P * (i % 4 + 1)],
+                lhsT=warm_codes[:].bitcast(FP8X4),
+                lhsT_scale=warm_scales[:],
+                rhs=warm_codes[:].bitcast(FP8X4),
+                rhs_scale=warm_scales[:],
+                start=True,
+                stop=True,
+            )
+
+        split_q(0, 0)
+        split_q(0, 1)
         vector_bank = psum.tile([P, P], BF16, name="turn_bank")
+        turn_q(0, 0)
         nc.tensor.transpose(vector_bank[:], vector_rows[:], ident_bf16[:])
+        turn_q(0, 1)
         nc.vector.tensor_copy(out=amp_cols[:], in_=vector_bank[:, 32 : 32 + R // P])
         nc.vector.tensor_scalar(out=neg_h[:], in0=vector_bank[:, :TILES], scalar1=-1.0, scalar2=None, op0=ALU.mult)
+        split_q(1, 0)
+        split_q(1, 1)
+        spread_amp(0)
         quantize_q(0, 0)
         quantize_q(0, 1)
         for half in (0, 1):
             turn_q(1, half)
             quantize_q(1, half)
-        for g in range(GROUPS):
-            spread_amp(g)
+        spread_amp(1)
         multiply(0, range(BASE_PASSES))
         multiply(2, range(BASE_PASSES))
         interleave_wo(0, 3, 4, True)
         for part in range(3):
             interleave_wo(0, part, 4, False)
+        spread_amp(2)
+        spread_amp(3)
+        split_q(2, 0)
+        split_q(2, 1)
         quantize_wo(0)
-        multiply(1, range(BASE_PASSES))
+        turn_q(2, 0)
+        turn_q(2, 1)
         multiply(0, [BASE_PASSES])
         multiply(2, [BASE_PASSES])
+        multiply(1, range(BASE_PASSES))
+        quantize_q(2, 0)
+        quantize_q(2, 1)
+        exponential(0)
+        exponential(2)
+        multiply(4, range(BASE_PASSES + 1))
         multiply(3, range(BASE_PASSES))
         interleave_wo(1, 3, 4, True)
         for part in range(3):
             interleave_wo(1, part, 4, False)
-        exponential(0)
-        exponential(2)
-        amplify(0)
+        exponential(4)
+        split_q(3, 0)
+        split_q(3, 1)
         quantize_wo(1)
-        turn_q(2, 0)
-        turn_q(2, 1)
+        turn_q(3, 0)
+        turn_q(3, 1)
         multiply(1, [BASE_PASSES])
         multiply(3, [BASE_PASSES])
-        amplify(2)
-        round_y(0)
-        quantize_q(2, 0)
-        quantize_q(2, 1)
+        multiply(5, range(BASE_PASSES + 1))
+        split_q(4, 0)
+        split_q(4, 1)
+        quantize_q(3, 0)
+        quantize_q(3, 1)
         exponential(1)
         exponential(3)
-        amplify(1)
-        round_y(2)
-        store_y(0, 2)
+        exponential(5)
 
+        to_amplify = [0, 2, 1, 3, 4] + list(range(5, UNITS - 1))
+        amplified, rounded_at, quantized, waiting = [], {}, set(), []
         next_pair = 0
-        waiting = []
-        for n in range(4, UNITS):
-            g, t = place(n)
-            first_phase = n < 2 * TILES
-            q_next = t + 1 if first_phase and n % 2 == 0 and t + 1 < TILES else None
+        turned = []
+
+        def epilogue_step(n):
+            unit = to_amplify.pop(0)
+            amplify(unit)
+            if waiting:
+                quantize_and_store(waiting.pop(0))
+            if amplified:
+                round_y(amplified[-1])
+                rounded_at[amplified[-1]] = n
+            amplified.append(unit)
+            if unit % 2 == 1:
+                store_y(unit - 1, 2)
+
+        def quantize_and_store(unit):
+            quantize_y(unit)
+            quantized.add(unit)
+            for phase, t0, t1, with_scales in PLANE_STORES:
+                units = range(2 * TILES * phase + 2 * t0, 2 * TILES * phase + 2 * t1)
+                if unit in units and all(m in quantized for m in units):
+                    store_words(phase, t0, t1)
+                    if with_scales:
+                        store_scales(phase, 0, t1, (nc.sync,) * 4)
+
+        for i in range(HEAD_EPILOGUES):
+            epilogue_step(5)
+        for n in range(6, UNITS):
+            q_next = Q_TURN.get(n)
             pairs = []
-            if (n % 2 == 0 if first_phase else n % 4 == 1 or n == UNITS - 1):
-                while next_pair + 1 <= (n - 3 if q_next is not None and n > 4 else n - 4):
-                    pairs.append(next_pair)
-                    next_pair += 2
+            while len(pairs) < Y_TURN.get(n, 0) and rounded_at.get(next_pair + 1, n) <= n - Y_LAG:
+                pairs.append(next_pair)
+                next_pair += 2
             if q_next is not None:
                 turn_q(q_next, 0)
                 turn_q(q_next, 1)
             for pair in pairs:
                 turn_y((pair, pair + 1))
             multiply(n, range(BASE_PASSES + 1))
-            amplify(n - 1)
-            if waiting:
-                quantize_y(waiting.pop(0))
-            round_y(1 if n == 4 else n - 2)
+            if n in Q_SPLIT:
+                split_q(Q_SPLIT[n], 0)
+                split_q(Q_SPLIT[n], 1)
+            epilogue_step(n)
             if q_next is not None:
                 quantize_q(q_next, 0)
                 quantize_q(q_next, 1)
-            for pair in pairs:
-                quantize_y(pair)
-            for pair in pairs:
-                if len(pairs) > 1:
-                    quantize_y(pair + 1)
+            if n in CATCH_UP:
+                epilogue_step(n)
+            turned.extend(pairs)
+            now, turned = turned[:2], turned[2:]
+            for pair in now:
+                quantize_and_store(pair)
+            for pair in now:
+                if len(now) > 1:
+                    quantize_and_store(pair + 1)
                 else:
                     waiting.append(pair + 1)
             if n in WO_ON_SCALAR:
@@ -318,30 +392,18 @@ def tile_positive_query_features_g5_kernel(
             if n in WO_ON_VECTOR:
                 part = WO_ON_VECTOR[n]
                 interleave_wo(2 + part // 4, part % 4, 4, False)
-            if n in (12, 14):
-                quantize_wo(2 + (n - 12) // 2)
+            if n in WO_QUANTIZE:
+                quantize_wo(WO_QUANTIZE[n])
             if n < UNITS - 1:
                 exponential(n)
-            if n % 2 == 0:
-                store_y(n - 2, 2)
-            if n == 22:
-                store_words(0, 4, TILES)
-                store_scales(0, 0, TILES, (nc.sync,) * 4)
-            if n == 14:
-                store_words(0, 0, 4)
-            if n == 26:
-                store_words(1, 0, 3)
-            if n == 29:
-                store_words(1, 3, 5)
-                store_scales(1, 0, 5, (nc.sync,) * 4)
+        assert next_pair == UNITS - 4 and not to_amplify
 
         last = UNITS - 1
         g, t = place(last)
         store_y(last - 1, 1)
         round_y(last - 1)
-        quantize_y(waiting.pop(0))
-        store_words(1, 5, 6)
-        exps[last] = work.tile([P, N], F32, name="exp")
+        quantize_and_store(waiting.pop(0))
+        exps[last] = work.tile([P, N], F32, name="exp", bufs=9)
         y_halves[last] = work.tile([P, 2, P, 2], BF16, name="y_halves", bufs=10, align_bytes=256)
         for half in (0, 1):
             c = slice(N // 2 * half, N // 2 * (half + 1))
@@ -363,4 +425,4 @@ def tile_positive_query_features_g5_kernel(
         store_words(1, 6, 7)
         quantize_y(last)
         store_words(1, 7, TILES)
-        store_scales(1, 5, TILES, (nc.scalar, nc.sync, nc.scalar, nc.sync))
+        store_scales(1, 4, TILES, (nc.scalar, nc.sync, nc.scalar, nc.sync))

from contextlib import ExitStack

import concourse.mybir as mybir
from concourse.masks import make_identity

T, KB, KO, R = 1024, 1536, 512, 2048
FLOPS = 2 * T * (KB + KO) * R

F32 = mybir.dt.float32
BF16 = mybir.dt.bfloat16
I32 = mybir.dt.int32
U32 = mybir.dt.uint32
U8 = mybir.dt.uint8
FP8X4 = mybir.dt.float8_e4m3fn_x4
FP4X4 = mybir.dt.float4_e2m1fn_x4
ACT = mybir.ActivationFunctionType
ALU = mybir.AluOpType

P = 128
N = 512
TILES = T // P
GROUPS = R // N
BASE_PASSES = KB // 512
UNITS = TILES * GROUPS
PHASES = GROUPS // 2
WARM_PASSES = 16
Q_TURN = {6: 4, 8: 5, 10: 6, 12: 7}
Q_SPLIT = {6: 5, 7: 6, 9: 7}
HEAD_EPILOGUES = 1
CATCH_UP = (16, 18, 19, 20)
Y_LAG = 2
ROUND_ON_SCALAR = (13, 15, 17, 19, 21)
Y_TURN = {10: 1, 12: 1, 17: 4, 22: 4, 26: 4, 29: 2, 31: 1}
PLANE_STORES = ((0, 0, 2, False), (0, 2, 4, False), (0, 4, 6, False), (0, 6, 8, True), (1, 0, 2, False), (1, 2, 4, True), (1, 4, 6, False))
WO_ON_SCALAR = {7: 0, 9: 1, 11: 2, 13: 4, 14: 5, 15: 6}
WO_ON_VECTOR = {11: 3, 13: 7}
WO_QUANTIZE = {14: 2, 15: 3}


def tile_positive_query_features_g5_kernel(
    tc, q_base, q_out, w_base_words, w_base_scales, w_out, half_norm, amp, out_0, out_1, out_2
):
    nc = tc.nc
    with ExitStack() as ctx:
        keep = ctx.enter_context(tc.tile_pool(name="keep", bufs=1))
        work = ctx.enter_context(tc.tile_pool(name="work", bufs=4))
        psum = ctx.enter_context(tc.psum_pool(name="psum", bufs=4))
        ctx.enter_context(tc.manual_schedule())

        def kept(name, count, shape, dtype):
            return [keep.tile(shape, dtype, name=name + str(i), align_bytes=256) for i in range(count)]

        ident = keep.tile([P, P], F32, align_bytes=256)
        ident_bf16 = keep.tile([P, P], BF16, align_bytes=256)
        vector_rows = keep.tile([P, P], BF16, align_bytes=256)
        amp_cols = keep.tile([P, R // P], BF16, align_bytes=256)
        neg_h = keep.tile([P, TILES], F32, align_bytes=256)
        table_in = keep.tile([P, 1], F32, align_bytes=256)
        table_out = keep.tile([P, 1], F32, align_bytes=256)
        q_raw = kept("q_raw", TILES, [P, KB + KO], BF16)
        q_codes = kept("q_codes", TILES, [P, 4 * P], U32)
        q_scales = kept("q_scales", TILES, [P, 4 * P], U8)
        wb_words = kept("wb_words", GROUPS, [P, BASE_PASSES, 2 * N], U8)
        wb_scales = kept("wb_scales", 2, [P, BASE_PASSES, N], U8)
        wb_scales_late = keep.tile([P, BASE_PASSES, 2 * N], U8, align_bytes=256)
        wo_raw = kept("wo_raw", GROUPS, [P, 4, N], BF16)
        wo_grouped = kept("wo_grouped", GROUPS, [P, N, 4], BF16)
        wo_codes = kept("wo_codes", GROUPS, [P, N], U32)
        wo_scales = kept("wo_scales", GROUPS, [P, N], U8)
        amp_all = kept("amp_all", GROUPS, [P, N], BF16)
        y_codes = kept("y_codes", PHASES, [P, 2, T], U32)
        y_scales = kept("y_scales", PHASES, [P, T], U8)

        warm_in = keep.tile([P, 4 * P], BF16, align_bytes=256)
        warm_codes = keep.tile([P, P], U32, align_bytes=256)
        warm_scales = keep.tile([P, P], U8, align_bytes=256)

        acc, exps, ys, y_halves, q_halves, grouped = {}, {}, {}, {}, {}, {}

        def cols(g):
            return slice(N * g, N * (g + 1))

        def place(n):
            phase, rest = divmod(n, 2 * TILES)
            return 2 * phase + rest % 2, rest // 2

        def load_q(t):
            rows = slice(P * t, P * (t + 1))
            nc.sync.dma_start(out=q_raw[t][:, :KB], in_=q_base[rows, :])
            nc.sync.dma_start(out=q_raw[t][:, KB:], in_=q_out[rows, :])

        def load_wb_scales(plane, columns):
            for quad in range(4):
                nc.sync.dma_start(
                    out=plane[32 * quad : 32 * quad + 4, :, :].bitcast(I32),
                    in_=w_base_scales[:, 4 * quad : 4 * quad + 4, columns].rearrange("c r n -> r c n").bitcast(I32),
                )

        def load_wb_words(g):
            nc.sync.dma_start(
                out=wb_words[g][:].bitcast(I32),
                in_=w_base_words[:, :, 2 * N * g : 2 * N * (g + 1)].rearrange("c p n -> p c n").bitcast(I32),
            )

        def load_wo(g):
            nc.sync.dma_start(out=wo_raw[g][:], in_=w_out[:, cols(g)].rearrange("(p j) n -> p j n", j=4))

        def spread_amp(g):
            bank = psum.tile([P, 4, P], BF16, name="turn_bank")
            for i in range(4):
                column = amp_cols[:, 4 * g + i : 4 * g + i + 1]
                nc.tensor.transpose(bank[:, i, :], column.to_broadcast([P, P]), ident_bf16[:])
            nc.scalar.copy(out=amp_all[g][:], in_=bank[:].rearrange("p i n -> p (i n)"))

        def interleave_wo(g, part, parts, on_scalar):
            width = N // parts
            c = slice(width * part, width * (part + 1))
            dst = wo_grouped[g][:, c, :].rearrange("p (c i) t -> p c t i", i=4)
            src = wo_raw[g][:, :, c].rearrange("p t (c i) -> p c t i", i=4)
            if on_scalar:
                nc.scalar.copy(out=dst, in_=src)
            else:
                nc.vector.tensor_copy(out=dst, in_=src)

        def quantize_wo(g):
            nc.vector.quantize_mx(
                out=wo_codes[g][:].bitcast(FP8X4),
                scales=wo_scales[g][:],
                in_=wo_grouped[g][:].rearrange("p n t -> p (n t)"),
            )

        def turn(key, blocks):
            count = len(blocks) // 2
            bank = psum.tile([P, 2, 2, P], F32, name="turn_bank")
            for i, block in enumerate(blocks):
                nc.tensor.transpose(bank[:, i // 2, i % 2, :], block, ident[:])
            tile = work.tile([P, 2, P, 4], BF16, name="turned", align_bytes=256)
            nc.scalar.copy(
                out=tile[:, :count].bitcast(F32),
                in_=bank[:, :count].rearrange("p c u r -> p c r u"),
            )
            grouped[key] = tile

        def split_q(t, half):
            words = q_raw[t][:].bitcast(F32)[:, 4 * P * half : 4 * P * (half + 1)]
            q_halves[t, half] = work.tile([P, 2, 2, P], F32, name="q_halves", bufs=6, align_bytes=256)
            nc.vector.tensor_copy(out=q_halves[t, half][:], in_=words.rearrange("p (c m u) -> p c u m", c=2, u=2))

        def turn_q(t, half):
            turn(("q", t, half), [q_halves[t, half][:, c, u, :] for c in (0, 1) for u in (0, 1)])

        def quantize_q(t, half):
            c = slice(2 * P * half, 2 * P * (half + 1))
            nc.vector.quantize_mx(out=q_codes[t][:, c].bitcast(FP8X4), scales=q_scales[t][:, c], in_=grouped["q", t, half][:].rearrange("p c r t -> p (c r t)"))

        def multiply(n, passes):
            g, t = place(n)
            if n not in acc:
                acc[n] = psum.tile([P, N], F32, name="acc")
            for c in passes:
                q_cols = slice(P * c, P * (c + 1))
                if c < BASE_PASSES:
                    rhs = wb_words[g][:, c, :].bitcast(FP4X4)
                    rhs_scale = wb_scales[g][:, c, :] if g < 2 else wb_scales_late[:, c, cols(g - 2)]
                else:
                    rhs = wo_codes[g][:].bitcast(FP8X4)
                    rhs_scale = wo_scales[g][:]
                nc.tensor.matmul_mx(
                    out=acc[n][:],
                    lhsT=q_codes[t][:, q_cols].bitcast(FP8X4),
                    lhsT_scale=q_scales[t][:, q_cols],
                    rhs=rhs,
                    rhs_scale=rhs_scale,
                    start=(c == 0),
                    stop=(c == BASE_PASSES),
                )

        def exponential(n):
            g, t = place(n)
            exps[n] = work.tile([P, N], F32, name="exp", bufs=9)
            nc.scalar.activation(out=exps[n][:], in_=acc[n][:], func=ACT.Exp, bias=neg_h[:, t : t + 1])

        def amplify(n):
            g, t = place(n)
            if n // 2 not in ys:
                ys[n // 2] = work.tile([P, 2, N], F32, name="y", bufs=7)
            nc.vector.tensor_tensor(out=ys[n // 2][:, n % 2, :], in0=exps[n][:], in1=amp_all[g][:], op=ALU.mult)

        def store_y(n, count):
            g, t = place(n)
            nc.sync.dma_start(
                out=out_0[P * t : P * (t + 1), N * g : N * (g + count)],
                in_=ys[n // 2][:, n % 2 : n % 2 + count, :].rearrange("p a n -> p (a n)"),
            )

        def round_y(n):
            y_halves[n] = work.tile([P, 2, P, 2], BF16, name="y_halves", bufs=10, align_bytes=256)
            copy = nc.scalar.copy if n in ROUND_ON_SCALAR else nc.vector.tensor_copy
            copy(out=y_halves[n][:], in_=ys[n // 2][:, n % 2, :].rearrange("p (m u e) -> p u m e", u=2, e=2))

        def turn_y(units):
            blocks = [y_halves[m][:, u].rearrange("p m e -> p (m e)").bitcast(F32) for m in units for u in (0, 1)]
            turn("y", blocks)
            for i, m in enumerate(units):
                grouped["y", m] = grouped["y"][:, i]

        def quantize_y(n):
            g, t = place(n)
            c = slice(P * t, P * (t + 1))
            nc.vector.quantize_mx(
                out=y_codes[g // 2][:, g % 2, c].bitcast(FP8X4),
                scales=y_scales[g // 2][4 * (g % 2) :, c],
                in_=grouped["y", n].rearrange("p r t -> p (r t)"),
            )

        def store_words(phase, t0, t1):
            words = out_1[2 * phase : 2 * phase + 2].rearrange("g p m t -> p g (m t)")
            nc.sync.dma_start(
                out=words[:, :, 4 * P * t0 : 4 * P * t1].bitcast(I32),
                in_=y_codes[phase][:, :, P * t0 : P * t1].bitcast(I32),
            )

        def store_scales(phase, t0, t1, queues):
            for quad, queue in enumerate(queues):
                queue.dma_start(
                    out=out_2[2 * phase : 2 * phase + 2, 4 * quad : 4 * quad + 4, P * t0 : P * t1].bitcast(I32),
                    in_=y_scales[phase][32 * quad : 32 * quad + 8, P * t0 : P * t1].bitcast(I32),
                )

        nc.vector.memset(warm_in[:].bitcast(I32), 0)
        nc.vector.memset(vector_rows[:], 0.0)
        nc.vector.quantize_mx(out=warm_codes[:].bitcast(FP8X4), scales=warm_scales[:], in_=warm_in[:])
        nc.vector.memset(wb_scales[0][:].bitcast(I32), 0)
        nc.vector.memset(table_in[:], 0.0)
        nc.vector.memset(wb_scales[1][:].bitcast(I32), 0)
        nc.vector.memset(wb_scales_late[:].bitcast(I32), 0)
        make_identity(nc, ident[:])
        make_identity(nc, ident_bf16[:])
        nc.scalar.activation(out=table_out[:], in_=table_in[:], func=ACT.Exp)

        load_q(0)
        nc.sync.dma_start(out=vector_rows[:TILES, :], in_=half_norm.rearrange("(a n) -> a n", n=P))
        nc.sync.dma_start(out=vector_rows[32 : 32 + R // P, :], in_=amp.rearrange("(a n) -> a n", n=P))
        load_q(1)
        load_wb_words(0)
        load_wb_scales(wb_scales[0], cols(0))
        load_wo(0)
        load_q(2)
        load_wb_words(1)
        load_wb_scales(wb_scales[1], cols(1))
        load_wo(1)
        for t in range(3, TILES):
            load_q(t)
        load_wo(2)
        load_wo(3)
        load_wb_scales(wb_scales_late, slice(2 * N, R))
        load_wb_words(2)
        load_wb_words(3)

        warm_bank = psum.tile([P, N], F32, name="acc")
        for i in range(WARM_PASSES):
            nc.tensor.matmul_mx(
                out=warm_bank[:, P * (i % 4) : P * (i % 4 + 1)],
                lhsT=warm_codes[:].bitcast(FP8X4),
                lhsT_scale=warm_scales[:],
                rhs=warm_codes[:].bitcast(FP8X4),
                rhs_scale=warm_scales[:],
                start=True,
                stop=True,
            )

        split_q(0, 0)
        split_q(0, 1)
        vector_bank = psum.tile([P, P], BF16, name="turn_bank")
        turn_q(0, 0)
        nc.tensor.transpose(vector_bank[:], vector_rows[:], ident_bf16[:])
        turn_q(0, 1)
        nc.vector.tensor_copy(out=amp_cols[:], in_=vector_bank[:, 32 : 32 + R // P])
        nc.vector.tensor_scalar(out=neg_h[:], in0=vector_bank[:, :TILES], scalar1=-1.0, scalar2=None, op0=ALU.mult)
        split_q(1, 0)
        split_q(1, 1)
        spread_amp(0)
        quantize_q(0, 0)
        quantize_q(0, 1)
        for half in (0, 1):
            turn_q(1, half)
            quantize_q(1, half)
        spread_amp(1)
        multiply(0, range(BASE_PASSES))
        multiply(2, range(BASE_PASSES))
        interleave_wo(0, 3, 4, True)
        for part in range(3):
            interleave_wo(0, part, 4, False)
        spread_amp(2)
        spread_amp(3)
        split_q(2, 0)
        split_q(2, 1)
        quantize_wo(0)
        turn_q(2, 0)
        turn_q(2, 1)
        multiply(0, [BASE_PASSES])
        multiply(2, [BASE_PASSES])
        multiply(1, range(BASE_PASSES))
        quantize_q(2, 0)
        quantize_q(2, 1)
        exponential(0)
        exponential(2)
        multiply(4, range(BASE_PASSES + 1))
        multiply(3, range(BASE_PASSES))
        interleave_wo(1, 3, 4, True)
        for part in range(3):
            interleave_wo(1, part, 4, False)
        exponential(4)
        split_q(3, 0)
        split_q(3, 1)
        quantize_wo(1)
        turn_q(3, 0)
        turn_q(3, 1)
        multiply(1, [BASE_PASSES])
        multiply(3, [BASE_PASSES])
        multiply(5, range(BASE_PASSES + 1))
        split_q(4, 0)
        split_q(4, 1)
        quantize_q(3, 0)
        quantize_q(3, 1)
        exponential(1)
        exponential(3)
        exponential(5)

        to_amplify = [0, 2, 1, 3, 4] + list(range(5, UNITS - 1))
        amplified, rounded_at, quantized, waiting = [], {}, set(), []
        next_pair = 0
        turned = []

        def epilogue_step(n):
            unit = to_amplify.pop(0)
            amplify(unit)
            if waiting:
                quantize_and_store(waiting.pop(0))
            if amplified:
                round_y(amplified[-1])
                rounded_at[amplified[-1]] = n
            amplified.append(unit)
            if unit % 2 == 1:
                store_y(unit - 1, 2)

        def quantize_and_store(unit):
            quantize_y(unit)
            quantized.add(unit)
            for phase, t0, t1, with_scales in PLANE_STORES:
                units = range(2 * TILES * phase + 2 * t0, 2 * TILES * phase + 2 * t1)
                if unit in units and all(m in quantized for m in units):
                    store_words(phase, t0, t1)
                    if with_scales:
                        store_scales(phase, 0, t1, (nc.sync,) * 4)

        for i in range(HEAD_EPILOGUES):
            epilogue_step(5)
        for n in range(6, UNITS):
            q_next = Q_TURN.get(n)
            pairs = []
            while len(pairs) < Y_TURN.get(n, 0) and rounded_at.get(next_pair + 1, n) <= n - Y_LAG:
                pairs.append(next_pair)
                next_pair += 2
            if q_next is not None:
                turn_q(q_next, 0)
                turn_q(q_next, 1)
            for pair in pairs:
                turn_y((pair, pair + 1))
            multiply(n, range(BASE_PASSES + 1))
            if n in Q_SPLIT:
                split_q(Q_SPLIT[n], 0)
                split_q(Q_SPLIT[n], 1)
            epilogue_step(n)
            if q_next is not None:
                quantize_q(q_next, 0)
                quantize_q(q_next, 1)
            if n in CATCH_UP:
                epilogue_step(n)
            turned.extend(pairs)
            now, turned = turned[:2], turned[2:]
            for pair in now:
                quantize_and_store(pair)
            for pair in now:
                if len(now) > 1:
                    quantize_and_store(pair + 1)
                else:
                    waiting.append(pair + 1)
            if n in WO_ON_SCALAR:
                part = WO_ON_SCALAR[n]
                interleave_wo(2 + part // 4, part % 4, 4, True)
            if n in WO_ON_VECTOR:
                part = WO_ON_VECTOR[n]
                interleave_wo(2 + part // 4, part % 4, 4, False)
            if n in WO_QUANTIZE:
                quantize_wo(WO_QUANTIZE[n])
            if n < UNITS - 1:
                exponential(n)
        assert next_pair == UNITS - 4 and not to_amplify

        last = UNITS - 1
        g, t = place(last)
        store_y(last - 1, 1)
        round_y(last - 1)
        quantize_and_store(waiting.pop(0))
        exps[last] = work.tile([P, N], F32, name="exp", bufs=9)
        y_halves[last] = work.tile([P, 2, P, 2], BF16, name="y_halves", bufs=10, align_bytes=256)
        for half in (0, 1):
            c = slice(N // 2 * half, N // 2 * (half + 1))
            nc.scalar.activation(out=exps[last][:, c], in_=acc[last][:, c], func=ACT.Exp, bias=neg_h[:, t : t + 1])
            nc.vector.tensor_tensor(
                out=y_halves[last][:, :, P // 2 * half : P // 2 * (half + 1), :],
                in0=exps[last][:, c].rearrange("p (m u e) -> p u m e", u=2, e=2),
                in1=amp_all[g][:, c].rearrange("p (m u e) -> p u m e", u=2, e=2),
                op=ALU.mult,
            )
        turn_y((last - 3, last - 2))
        turn_y((last - 1,))
        turn_y((last,))
        amplify(last)
        store_y(last, 1)
        quantize_y(last - 3)
        quantize_y(last - 1)
        quantize_y(last - 2)
        store_words(1, 6, 7)
        quantize_y(last)
        store_words(1, 7, TILES)
        store_scales(1, 4, TILES, (nc.scalar, nc.sync, nc.scalar, nc.sync))
